import numpy as np, ml_dtypes
CORES = [8,136,40,168]
N = 4
BF = ml_dtypes.bfloat16
def f(rng, *shape):
    return (rng.standard_normal(shape, dtype=np.float32) * np.exp2(rng.integers(-2, 3, shape[:-1] + (1,)))).astype(BF)
def wide(rng, *shape):
    v = f(rng, *shape).astype(np.float32); k = shape[:-2] + (1, shape[-1])
    return (v * np.exp2(rng.integers(-6, 7, k)) * (rng.random(k) > 0.0625)).astype(BF)
def gentries(a):
    return np.ascontiguousarray(a.reshape(8, 16, -1).transpose(0, 2, 1)).reshape(8, -1)
def gtable(e):
    e = np.asarray(e); return np.ascontiguousarray(e.reshape(8, -1, 16).transpose(0, 2, 1)).reshape(128, -1).astype(np.int32)
E, D, CAP, S, P = 4096, 4, 256, 2, 5120
def setup_inputs(rng):
    mp = rng.integers(0, 8, (8, S)); mp[:, S - 1] = rng.permutation(8); i, j = rng.permutation(8)[:2]; mp[j, :S - 1] = mp[i, :S - 1]
    sh = (N, 8, D * E); pl = np.where(rng.random(sh) < 0.5, rng.integers(0, E, sh), rng.integers(E, P, sh)); se = rng.integers(0, E, (N, 8, N * CAP))
    return {"x": f(rng, N, 16, E), "mp": np.repeat(mp[None], N, 0).astype(np.int32),
            "src": np.stack([gtable(e) for e in pl]), "snd": np.stack([gtable(e) for e in se]),
            "bs": f(rng, N, 128, 1).astype(np.float32) * np.float32(0.25),
            "aw": rng.standard_normal((N, 16, 16), dtype=np.float32) * np.float32(0.5),
            "ab": rng.standard_normal((N, 16, 1), dtype=np.float32) * np.float32(0.25),
            "aq": np.clip(0.4 * rng.standard_normal((N, 16, 1)), -1, 1).astype(np.float32)}
def setup_inputs_full(rng):
    d = setup_inputs(rng)
    d["src"] = np.stack([gtable(np.stack([E + rng.permutation(D * E) % (N * CAP) for k in range(8)])) for r in range(N)])
    d["snd"] = np.stack([gtable(np.stack([np.concatenate([rng.permutation(E)[:CAP] for q in range(N)]) for k in range(8)])) for r in range(N)]); return d
def setup_inputs_edges(rng):
    d = setup_inputs(rng); ends = np.array([0, E - 1] + [E + q * CAP + i for q in range(N) for i in (0, CAP - 1)])
    pl = rng.choice(ends, (N, 8, D * E)); pl[:, rng.integers(0, 8)] = P - 1; se = rng.choice(np.array([0, E - 1]), (N, 8, N * CAP))
    d["src"] = np.stack([gtable(e) for e in pl]); d["snd"] = np.stack([gtable(e) for e in se]); return d
def setup_inputs_chains(rng):
    d = setup_inputs(rng); c = rng.choice(np.array([0, 7]), (3, S)); c[1, 0] = 0; c[2, 0] = 7; c[:, S - 1] = rng.permutation(8)[:3]; c[0] = c[0, S - 1]
    d["mp"] = np.repeat(c[rng.permutation(np.array([0, 0, 0, 1, 1, 2, 2, 2]))][None], N, 0).astype(np.int32); return d
def setup_inputs_dead(rng):
    d = setup_inputs(rng); k, z = rng.permutation(8)[:2]; d["bs"][:, 16 * k:16 * k + 16] = -4096; d["bs"][:, 16 * z:16 * z + 16] = 0
    g = int(np.flatnonzero(d["mp"][0, :, S - 1] != k)[rng.integers(0, 7)]); d["mp"][:, g, 0] = k; return d
def setup_inputs_spread(rng):
    d = setup_inputs(rng); d["x"] = wide(rng, N, 16, E); return d
def check_inputs(d):
    bad = []
    for a, n in (("src", P), ("snd", E), ("mp", 8)):
        if d[a].min() < 0 or d[a].max() >= n: bad.append("range of " + a)
    if (d["mp"] != d["mp"][:1]).any(): bad.append("mp is the same on all ranks")
    if not (np.abs(d["aq"]) <= 1).all(): bad.append("range of aq")
    for a in ("x", "bs", "aw", "ab", "aq"):
        if not np.isfinite(d[a].astype(np.float32)).all(): bad.append("finite " + a)
    return bad
def reference(x, mp, src, snd, bs, aw, ab, aq):
    h = np.repeat(x.astype(np.float64)[:, None], 8, axis=1)
    pl = np.stack([gentries(a) for a in src]); se = np.stack([gentries(a) for a in snd]).reshape(N, 8, N, CAP); b = bs.astype(np.float64).reshape(N, 8, 16, 1)
    for s in range(S):
        nh = np.zeros_like(h)
        for g in range(8):
            k = int(mp[0, g, s])
            for r in range(N):
                win = np.concatenate([h[r, g]] + [h[q, g][:, se[q, k, r]] for q in range(N)], axis=1)
                v = np.sum(win[:, pl[r, k]].reshape(16, D, E), axis=1)
                nh[r, g] = np.maximum(v * 2.0 ** -2 + b[r, k], 0)
        h = nh
    tot = np.zeros(8, np.float64)
    for r in range(N):
        for g in range(8):
            t = np.tanh(aw[r].astype(np.float64).T @ h[r, g] + ab[r].astype(np.float64))
            tot[g] += np.sum(aq[r].astype(np.float64) * t)
    w = np.exp(tot * 2.0 ** -14)
    y = np.einsum("g,rgce->rce", w, h)
    return {"y": y.astype(np.float32), "w": np.repeat(w[None, :, None], N, axis=0).astype(np.float32)}

@@ -1,0 +1,358 @@
+from concourse.bass import DstId, RemoteDMATransfer, IndirectOffsetOnAxis
+from concourse.mybir import AluOpType, AxisListType, ActivationFunctionType
+
+E, CAP, N = 4096, 256, 4
+P = E + N * CAP
+XP = 3072
+SCRATCH = {"aqd": ("dram", [128, 1], "float32"), "aql": ("dram", [4, 128, 1], "float32"),
+           "ps": ("psum", [128, 4096], "float32")}
+for _rows, _cols, _dt, _names in (
+        (128, 128, "bfloat16", "onesb permb"), (8, 128, "bfloat16", "c16 r16a r16 mpr0 mpr1"), (16, 128, "bfloat16", "lb"),
+        (16, 128, "float32", "l32 awr"), (128, 128, "float32", "cn ones bda bd perm0 perm1 awb q0 q1 q2 q3"),
+        (128, 1, "int32", "pio pm"), (128, 1, "float32", "pmf bst b0 b1 abc so st eo et wv"), (8, 2, "int32", "mpi"),
+        (8, 2, "bfloat16", "mpf"), (8, 2, "float32", "mpg"), (128, 2, "int32", "idx"), (16, 1, "float32", "abt"),
+        (16, 4, "float32", "aq16"), (16, XP, "bfloat16", "xs"), (128, 64, "int32", "snd0i snd1i"),
+        (128, 64, "uint16", "snd0 snd1"), (128, 1024, "int32", "l0i l1i"), (128, 1024, "uint16", "l0 l1"),
+        (128, P, "bfloat16", "w0"), (128, P, "float32", "w1"), (128, 3 * CAP, "bfloat16", "sb0"),
+        (128, 3 * CAP, "float32", "sb1"), (128, E, "bfloat16", "ga gb gg gd th"), (128, E, "float32", "a0 a1 h"),
+        (128, 48, "float32", "acc"), (128, 16, "float32", "ld ldo wm"), (128, 16, "bfloat16", "ldb"),
+        (128, 4, "float32", "aqs"), (128, 512, "float32", "yt")):
+    for _n in _names.split():
+        SCRATCH[_n] = ("sbuf", [_rows, _cols], _dt)
+SEMAPHORES = ["cV", "cS", "cP", "cG", "dx", "dx2", "dxr", "dsnd", "dmp", "dsrc", "daq", "dbs", "daw", "dql", "gi", "st0",
+              "st1", "dw", "aqa", "arr0", "arr1", "sca0", "sca1", "sca2", "sca3", "ac5", "ac6", "ac7", "loc"]
+
+CH = [(0, 256), (256, 256), (512, 512), (1024, 512), (1536, 512), (2048, 512), (2560, 512), (3072, 512), (3584, 256),
+      (3840, 128), (3968, 128)]
+TWO = (5, 6, 7)
+ORDER = {
+    "V": "0.0 0.1 2.1 0.2 2.2 1.1 0.3 1.2 3.1 1.3 2.3 1.r 4.1 3.2 4.2 3.3 5.2 4.3 5.3 6.2 8.1 6.3 7.2 9.1 7.3 9.2 8.2 10.1 "
+         "8.3 10.2 8.r 10.3 9.3 10.r 9.r",
+    "S": "2.0 5.0 1.0 3.0 5.1 4.0 6.0 0.r 6.1 2.r 7.1 7.0 0.t 10.0 9.0 3.r 1.t 8.0 4.r 5.r 3.t 2.t 6.r 4.t 7.r 6.t 5.t 7.t "
+         "8.t 10.t 9.t",
+    "P": "0.m 1.m 2.m 3.m 4.m 5.m 6.m 7.m 8.m 10.m 9.m",
+    "G": "5.+ 6.+ 7.+"}
+NB = 6
+
+
+def rank_program(g, core, T, topo):
+    r = T.rank_of(core)
+    if r is None:
+        return
+    A, F = AluOpType, ActivationFunctionType
+    queues = {"V": g.vector, "S": g.scalar, "P": g.tensor, "G": g, "Y": g.sync}
+    cnt = {"V": 0, "S": 0, "P": 0, "G": 0}
+    seen = {}
+    total = {}
+
+    def wait(q, *tokens):
+        for t in tokens:
+            s, v = t
+            if seen.get((q, s), 0) < v:
+                queues[q].wait_ge(T.sem[s], v)
+                seen[(q, s)] = v
+
+    def done(q, ins):
+        ins.then_inc(T.sem["c" + q], 1)
+        cnt[q] += 1
+        return ("c" + q, cnt[q])
+
+    def dma(q, sem, out, in_):
+        queues[q].dma_start(out, in_).then_inc(T.sem[sem], 16)
+        total[sem] = total.get(sem, 0) + 16
+        return (sem, total[sem])
+
+    peers = [T.cores[(r + k) % N] for k in (1, 2, 3)]
+    ranks = [(r + k) % N for k in (1, 2, 3)]
+    eng = len(topo.engines(core, peers[0]))
+    nloc = [0]
+
+    def send(out, in_, sem, dst):
+        rid, pid = topo.addr(dst, core)
+        g.remote_dma(out, in_, T.sem[sem], T.sem.loc, pid, rid, topo.mask(core, dst))
+        nloc[0] += len(topo.engines(core, dst))
+
+    def send_all(out, in_, sem):
+        ids = []
+        for d in peers:
+            rid, pid = topo.addr(d, core)
+            ids.append(DstId(rid=rid, pnc=pid))
+        g.remote_dma_fused([RemoteDMATransfer(dst_ids=ids, dma_engine_mask=topo.mask(core, peers[0]),
+                                              remote_sem=T.sem[sem], src=in_, dsts=[out, out, out])], local_sem=T.sem.loc)
+        nloc[0] += eng
+
+    def bank(b, n, o=0):
+        return T.ps[:, 512 * b + o:512 * b + o + n]
+
+    def gather(q, out, win, off, deps):
+        wait(q, *deps)
+        if q == "V":
+            return done("V", g.vector.tensor_copy(out, win.indirect(off)))
+        return done("S", g.scalar.activation(out, win.indirect(off), F.Identity))
+
+    tx = [dma("Y", "dx", T.xs[:, 0:XP // 2], T.x[:, 0:XP // 2]), dma("Y", "dx2", T.xs[:, XP // 2:XP], T.x[:, XP // 2:XP])]
+    dma("S", "daq", T.aqd[0:16, :], T.aq[:])
+    taq = dma("S", "daq", T.aqd[16:128, :], T.bs[16:128, :])
+    tsnd = dma("Y", "dsnd", T.snd0i[:], T.snd[:])
+    tmp = dma("S", "dmp", T.mpi[:], T.mp[:])
+    for k in range(8):
+        txr = dma("YS"[k % 2], "dxr", T.w0[16 * k:16 * k + 16, XP:E], T.x[:, XP:E])
+    tsrc = dma("Y", "dsrc", T.l0i[:], T.src[:])
+    tbs = dma("Y", "dbs", T.bst[:], T.bs[:])
+    dma("Y", "daw", T.abt[:], T.ab[:])
+    for k in range(8):
+        taw = dma("Y", "daw", T.awr[:, 16 * k:16 * k + 16], T.aw[:])
+
+    v1 = done("V", g.vector.memset(T.onesb[:], 1.0))
+    v2 = done("V", g.vector.memset(T.c16[:], 16.0))
+    v3 = done("V", g.vector.memset(T.ones[:], 1.0))
+    wait("G", v1)
+    tlb = done("G", g.affine_select(T.lb[:], T.onesb[0:16, :], [[0, 8], [1, 16]], A.is_equal, 0.0, 0, -1))
+    wait("G", v2)
+    t = done("G", g.affine_select(T.r16a[:], T.c16[:], [[1, 128]], A.is_ge, 0.0, 0, -16))
+    wait("G", t)
+    tr16 = done("G", g.affine_select(T.r16[:], T.r16a[:], [[-1, 128]], A.is_ge, 0.0, 15, 16))
+    tpio = done("G", g.iota(T.pio[:], [[0, 1]], 0, 1))
+    tcn = done("G", g.iota(T.cn[:], [[0, 8], [-1, 16]], 0, 1, allow_small_or_imprecise_dtypes=True))
+    wait("G", taq)
+    send_all(T.aql[r], T.aqd[:], "aqa")
+
+    wait("P", tlb)
+    px = []
+    for b in range(XP // 512):
+        wait("P", tx[512 * b >= XP // 2])
+        px.append(done("P", g.tensor.matmul(bank(b, 512), T.lb[:], T.xs[:, 512 * b:512 * b + 512], True, True)))
+    wait("V", tsnd)
+    vsnd = done("V", g.vector.tensor_copy(T.snd0[:], T.snd0i[:]))
+    xe = []
+    for b in range(XP // 512):
+        q = "VS"[b % 2]
+        wait(q, px[b])
+        o = T.w0[:, 512 * b:512 * b + 512]
+        if q == "V":
+            xe.append(done("V", g.vector.tensor_copy(o, bank(b, 512))))
+        else:
+            xe.append(done("S", g.scalar.activation(o, bank(b, 512), F.Identity)))
+
+    def exchange(win, sb, lists, deps, sem):
+        w = win[:, 0:E]
+        tk = []
+        for i, q, o, n in ((0, "V", 0, 128), (0, "S", 128, 128), (1, "V", 0, 256), (2, "S", 0, 256)):
+            c0 = 16 * ranks[i] + o // 16
+            tk.append((i, gather(q, sb[:, CAP * i + o:CAP * i + o + n], w, lists[:, c0:c0 + n // 16], deps)))
+        own = gather("S", win[:, E + CAP * r:E + CAP * r + CAP], w, lists[:, 16 * r:16 * r + 16], deps)
+        for i in range(3):
+            wait("G", *[t for j, t in tk if j == i])
+            send(win[:, E + CAP * r:E + CAP * r + CAP], sb[:, CAP * i:CAP * i + CAP], sem, peers[i])
+        return own
+
+    own0 = exchange(T.w0, T.sb0, T.snd0, xe + [vsnd, txr], "arr0")
+
+    wait("V", tmp)
+    done("V", g.vector.tensor_copy(T.mpf[:], T.mpi[:]))
+    t3 = done("V", g.vector.tensor_copy(T.mpg[:], T.mpi[:]))
+    wait("V", tpio)
+    t2 = done("V", g.vector.tensor_scalar(T.pm[:], T.pio[:], 15, None, A.bitwise_and))
+    wait("V", t3)
+    tm = [done("V", g.vector.tensor_scalar(T.mpr0[:], T.onesb[0:8, :], T.mpg[:, 0:1], None, A.mult)),
+          done("V", g.vector.tensor_scalar(T.mpr1[:], T.onesb[0:8, :], T.mpg[:, 1:2], None, A.mult))]
+    wait("V", t2)
+    tpm = done("V", g.vector.tensor_copy(T.pmf[:], T.pm[:]))
+    wait("P", tr16, *tm)
+    wait("P", *xe)
+    pidx = done("P", g.tensor.matmul(bank(2, 2), T.r16[:], T.mpf[:], True, True))
+    pa = done("P", g.tensor.matmul(bank(0, 128), T.mpr0[:], T.r16[:], True, True))
+    wait("V", pidx, tpm)
+    tidx = done("V", g.vector.tensor_scalar(T.idx[:], bank(2, 2), T.pmf[:], None, A.add))
+    wait("V", tcn, pa)
+    t = done("V", g.vector.tensor_tensor(T.perm0[:], bank(0, 128), T.cn[:], A.is_equal))
+    wait("V", tsrc)
+    vl0 = done("V", g.vector.tensor_copy(T.l0[:], T.l0i[:]))
+    wait("S", t)
+    tpb = done("S", g.scalar.activation(T.permb[:], T.perm0[:], F.Identity, scale=0.0625))
+    wait("P", tbs, t)
+    t = done("P", g.tensor.matmul(bank(3, 1), T.perm0[:], T.bst[:], True, True))
+    wait("S", t)
+    tb0 = done("S", g.scalar.activation(T.b0[:], bank(3, 1), F.Identity, scale=0.25))
+    wait("G", tidx)
+    for o, tab in ((T.snd1i, T.snd), (T.l1i, T.src)):
+        g.indirect_dma_start(o[:], None, tab[:], IndirectOffsetOnAxis(ap=T.idx[:, 1:2], axis=0),
+                             bounds_check=127).then_inc(T.sem.gi, 16)
+    wait("G", v3)
+    t = done("G", g.affine_select(T.bda[:], T.ones[:], [[-16, 8], [0, 16]], A.is_ge, 0.0, 0, 1))
+    wait("G", t)
+    tbd = done("G", g.affine_select(T.bd[:], T.bda[:], [[16, 8], [0, 16]], A.is_ge, 0.0, 15, -1))
+    wait("Y", taq)
+    dma("Y", "dql", T.aq16[:, r:r + 1], T.aqd[0:16, :])
+    wait("Y", ("aqa", 3 * eng))
+    for q in ranks:
+        tql = dma("Y", "dql", T.aq16[:, q:q + 1], T.aql[q, 0:16, :])
+
+    bufs = (T.ga, T.gb, T.gg, T.gd)
+    chunks = [(0, 1024), (1024, 1024), (2048, 1024), (3072, 512), (3584, 256), (3840, 128), (3968, 128)]
+    arrived = [("arr0", 3 * eng), own0, vl0, txr] + xe
+    pend, h0, npiece = [], [], 0
+
+    def evac(p):
+        e0, n, b, q, tk = p
+        o, i = T.w1[:, e0:e0 + n], bank(b, n)
+        wait(q, tk, tb0)
+        if q == "V":
+            h0.append(done("V", g.vector.tensor_scalar(o, i, T.b0[:], 0.0, A.add, A.max)))
+        else:
+            h0.append(done("S", g.scalar.activation(o, i, F.Relu, bias=T.b0[:])))
+
+    for e0, n in chunks:
+        tk = [gather("VVSS"[d], bufs[d][:, e0:e0 + n], T.w0[:],
+                     T.l0[:, 256 * d + e0 // 16:256 * d + (e0 + n) // 16], arrived) for d in (0, 2, 1, 3)]
+        for p in pend:
+            evac(p)
+        pend = []
+        for c0 in range(e0, e0 + n, 512):
+            m = min(512, e0 + n - c0)
+            b = npiece % 8
+            wait("P", tpb, tb0)
+            if npiece >= 8:
+                wait("P", h0[npiece - 8])
+            for i, d in enumerate((0, 2, 1, 3)):
+                wait("P", tk[i])
+                x = done("P", g.tensor.matmul(bank(b, m), T.permb[:], bufs[d][:, c0:c0 + m], i == 0, i == 3))
+            pend.append((c0, m, b, "VS"[npiece % 2], x))
+            npiece += 1
+        if e0 == 1024:
+            wait("V", ("gi", 32))
+            vs1 = done("V", g.vector.tensor_copy(T.snd1[:], T.snd1i[:]))
+    for p in pend:
+        evac(p)
+
+    own1 = exchange(T.w1, T.sb1, T.snd1, h0 + [vs1], "arr1")
+
+    tl32 = done("V", g.vector.tensor_copy(T.l32[:], T.lb[:]))
+    vl1 = done("V", g.vector.tensor_copy(T.l1[:], T.l1i[:]))
+    wait("P", taw, tql, tl32)
+    wait("P", *h0)
+    p1 = done("P", g.tensor.matmul(bank(0, 128), T.l32[:], T.awr[:], True, True))
+    p2 = done("P", g.tensor.matmul(bank(1, 1), T.l32[:], T.abt[:], True, True))
+    p3 = done("P", g.tensor.matmul(bank(2, 16), T.l32[:], T.l32[:, 0:16], True, True))
+    p4 = done("P", g.tensor.matmul(bank(3, 4), T.l32[:], T.aq16[:], True, True))
+    p5 = done("P", g.tensor.matmul(bank(4, 128), T.mpr1[:], T.r16[:], True, True))
+    wait("S", p3)
+    tldb = done("S", g.scalar.activation(T.ldb[:], bank(2, 16), F.Tanh, scale=16.0))
+    wait("V", p5)
+    t = done("V", g.vector.tensor_tensor(T.perm1[:], bank(4, 128), T.cn[:], A.is_equal))
+    wait("P", t)
+    p6 = done("P", g.tensor.matmul(bank(5, 1), T.perm1[:], T.bst[:], True, True))
+    wait("V", p4)
+    t = done("V", g.vector.tensor_scalar(T.aqs[:], bank(3, 4), 2.0 ** -14, None, A.mult))
+    wait("V", p1, tbd)
+    tawb = done("V", g.vector.tensor_tensor(T.awb[:], bank(0, 128), T.bd[:], A.mult))
+    wait("V", p2)
+    tabc = done("V", g.vector.tensor_copy(T.abc[:], bank(1, 1)))
+    wait("V", tldb)
+    tl = done("V", g.vector.tensor_scalar(T.ld[:], T.ldb[:], -1.0, 1024.0, A.add, A.mult))
+    wait("V", p6)
+    tb1 = done("V", g.vector.tensor_copy(T.b1[:], bank(5, 1)))
+    wait("S", t, tbd)
+    qs = (T.q0, T.q1, T.q2, T.q3)
+    for q in range(N):
+        tq = done("S", g.scalar.activation(qs[q][:], T.bd[:], F.Identity, scale=T.aqs[:, q:q + 1]))
+
+    arrived = [("arr1", 3 * eng), own1, vl1] + h0
+    ready = {}
+    pord = [int(x.split(".")[0]) for x in ORDER["P"].split()]
+
+    def needs(j, k):
+        if k == "0" or k == "1" and j in TWO:
+            return []
+        if k == "+":
+            return [(j, "0"), (j, "1")]
+        if k == "m":
+            i = pord.index(j)
+            return [(j, "r")] + ([(pord[i - NB], "t")] if i >= NB else [])
+        before = {"1": "0", "2": "+" if j in TWO else "1", "3": "2", "r": "3", "t": "m"}
+        return [(j, before[k])]
+
+    def emit(q, j, k):
+        e0, n = CH[j]
+        s = slice(e0, e0 + n)
+        wait(q, *[ready[x] for x in needs(j, k)])
+        sums = (T.a0, T.a0, T.a1, T.a0) if j in TWO else (T.a0, T.a1, T.a0, T.a1)
+        if k in "0123":
+            off = T.l1[:, 256 * int(k) + e0 // 16:256 * int(k) + (e0 + n) // 16]
+            if k == "0" or k == "1" and j in TWO:
+                return gather(q, (T.a0 if k == "0" else T.h)[:, s], T.w1[:], off, arrived)
+            wait("V", *arrived)
+            return done("V", g.vector.tensor_tensor(sums[int(k)][:, s], T.w1[:].indirect(off), sums[int(k) - 1][:, s], A.add))
+        if k == "+":
+            sem = "ac%d" % j
+            g.dma_start(T.a0[:, s], T.h[:, s], accum_op=A.add).then_inc(T.sem[sem], 16)
+            total[sem] = 16
+            return (sem, 16)
+        if k == "r":
+            wait(q, tb1)
+            if q == "V":
+                return done("V", g.vector.tensor_scalar(T.h[:, s], sums[3][:, s], T.b1[:], 0.0, A.add, A.max))
+            return done("S", g.scalar.activation(T.h[:, s], sums[3][:, s], F.Relu, bias=T.b1[:]))
+        b = bank(pord.index(j) % NB, n)
+        if k == "m":
+            wait("P", tawb, tb1, tq)
+            return done("P", g.tensor.matmul(b, T.awb[:], T.h[:, s], True, True))
+        wait("S", tabc)
+        return done("S", g.scalar.activation(T.th[:, s], b, F.Tanh, bias=T.abc[:],
+                                             accum_out=T.acc[:, 12 * r + j:12 * r + j + 1]))
+
+    left = {q: [(int(x.split(".")[0]), x.split(".")[1]) for x in ORDER[q].split()] for q in "VSPG"}
+    while any(left.values()):
+        for q in "VSPG":
+            while left[q] and all(x in ready for x in needs(*left[q][0])):
+                x = left[q].pop(0)
+                ready[x] = last = emit(q, *x)
+
+    nch = len(CH)
+    last = ("cS", cnt["S"])
+    wait("G", last)
+    mine = T.acc[:, 12 * r:12 * r + nch]
+    send_all(mine, mine, "sca%d" % r)
+    wait("P", last, tq)
+    p1 = done("P", g.tensor.matmul(bank(6, nch), qs[r][:], mine, True, True))
+    for i, q in enumerate(ranks[::-1]):
+        wait("P", ("sca%d" % q, eng))
+        p2 = done("P", g.tensor.matmul(bank(7, nch), qs[q][:], T.acc[:, 12 * q:12 * q + nch], i == 0, i == 2))
+    wait("V", p1)
+    t = done("V", g.vector.tensor_reduce(T.so[:], bank(6, nch), AxisListType.X, A.add))
+    wait("S", t)
+    teo = done("S", g.scalar.activation(T.eo[:], T.so[:], F.Exp))
+    wait("V", t, tl)
+    tld = done("V", g.vector.tensor_scalar(T.ldo[:], T.ld[:], T.so[:], None, A.add))
+    wait("V", p2)
+    t = done("V", g.vector.tensor_reduce(T.st[:], bank(7, nch), AxisListType.X, A.add))
+    wait("S", t, tld)
+    twm = done("S", g.scalar.activation(T.wm[:], T.ldo[:], F.Exp, bias=T.st[:]))
+    tet = done("S", g.scalar.activation(T.et[:], T.st[:], F.Exp))
+    wait("V", tet, teo)
+    twv = done("V", g.vector.tensor_tensor(T.wv[:], T.et[:], T.eo[:], A.mult))
+
+    wait("P", twm)
+    tz = []
+    for hb in (0, 1):
+        for b in range(8):
+            if hb:
+                wait("P", tz[b])
+            for k in (0, 1):
+                c0 = 1024 * (2 * hb + k)
+                py = done("P", g.tensor.matmul(bank(b, 16, 16 * k), T.h[:, c0 + b:c0 + 1024:8], T.wm[:], True, True))
+            wait("V", py)
+            ty = done("V", g.vector.transpose(T.yt[:, 256 * hb + b:256 * hb + 256:8], bank(b, 32)))
+            tz.append(ty)
+        for a in range(4):
+            for k in (0, 1):
+                q = "YS"[k]
+                wait(q, ty)
+                c0 = 1024 * (2 * hb + k) + 256 * a
+                dma(q, "st%d" % hb, T.y[:, c0:c0 + 256], T.yt[32 * a + 16 * k:32 * a + 16 * k + 16, 256 * hb:256 * hb + 256])
+        if hb == 0:
+            wait("Y", twv)
+            dma("Y", "dw", T.w[:], T.wv[0:128:16, :])
+
+    wait("G", ("loc", nloc[0]), ("gi", 32), *total.items())
+    wait("G", *[("c" + q, n) for q, n in cnt.items()])

@@ -3,51 +3,64 @@ from concourse.mybir import AluOpType, AxisListType, ActivationFunctionType
 
 E, CAP, N = 4096, 256, 4
 P = E + N * CAP
-XP = 3072
+XP = 2560
 SCRATCH = {"aqd": ("dram", [128, 1], "float32"), "aql": ("dram", [4, 128, 1], "float32"),
-           "ps": ("psum", [128, 4096], "float32")}
+           "ps": ("psum", [128, 4096], "float32"), "l1": ("sbuf", [128, 8, 128], "uint16"),
+           "l0": ("sbuf", [128, 8, 128], "uint16"), "gb": ("sbuf", [128, 8, 2048], "bfloat16"),
+           "a0": ("sbuf", [128, 8, 1024], "float32")}
 for _rows, _cols, _dt, _names in (
-        (128, 128, "bfloat16", "onesb permb"), (8, 128, "bfloat16", "c16 r16a r16 mpr0 mpr1"), (16, 128, "bfloat16", "lb"),
-        (16, 128, "float32", "l32 awr"), (128, 128, "float32", "cn ones bda bd perm0 perm1 awb q0 q1 q2 q3"),
-        (128, 1, "int32", "pio pm"), (128, 1, "float32", "pmf bst b0 b1 abc so st eo et wv"), (8, 2, "int32", "mpi"),
-        (8, 2, "bfloat16", "mpf"), (8, 2, "float32", "mpg"), (128, 2, "int32", "idx"), (16, 1, "float32", "abt"),
+        (128, 128, "bfloat16", "onesb permb"), (8, 128, "bfloat16", "c16 r16 mpr0 mpr1"), (16, 128, "bfloat16", "lb"),
+        (16, 128, "float32", "l32 ones"), (128, 128, "float32", "cn perm0 perm1 awb q0 q1 q2 q3"),
+        (128, 1, "int32", "pio pm idx"), (128, 1, "float32", "pmf bst b0 b1 abc so st eo et wv"), (8, 2, "int32", "mpi"),
+        (8, 2, "bfloat16", "mpf"), (8, 2, "float32", "mpg"),
         (16, 4, "float32", "aq16"), (16, XP, "bfloat16", "xs"), (128, 64, "int32", "snd0i snd1i"),
-        (128, 64, "uint16", "snd0 snd1"), (128, 1024, "int32", "l0i l1i"), (128, 1024, "uint16", "l0 l1"),
+        (128, 64, "uint16", "snd0 snd1"), (128, 1024, "int32", "l0i l1i"),
         (128, P, "bfloat16", "w0"), (128, P, "float32", "w1"), (128, 3 * CAP, "bfloat16", "sb0"),
-        (128, 3 * CAP, "float32", "sb1"), (128, E, "bfloat16", "ga gb gg gd th"), (128, E, "float32", "a0 a1 h"),
-        (128, 48, "float32", "acc"), (128, 16, "float32", "ld ldo wm"), (128, 16, "bfloat16", "ldb"),
+        (128, 3 * CAP, "float32", "sb1"), (128, E, "bfloat16", "th"), (128, E, "float32", "a1 h"),
+        (128, 64, "float32", "acc"), (128, 16, "float32", "ld ldo wm"), (128, 16, "bfloat16", "ldb"),
         (128, 4, "float32", "aqs"), (128, 512, "float32", "yt")):
     for _n in _names.split():
         SCRATCH[_n] = ("sbuf", [_rows, _cols], _dt)
-SEMAPHORES = ["cV", "cS", "cP", "cG", "dx", "dx2", "dxr", "dsnd", "dmp", "dsrc", "daq", "dbs", "daw", "dql", "gi", "st0",
-              "st1", "dw", "aqa", "arr0", "arr1", "sca0", "sca1", "sca2", "sca3", "ac5", "ac6", "ac7", "loc"]
 
-CH = [(0, 256), (256, 256), (512, 512), (1024, 512), (1536, 512), (2048, 512), (2560, 512), (3072, 512), (3584, 256),
+P0 = [(512 * _b, 512) for _b in range(7)] + [(3584, 448), (4032, 64)]
+G1 = [(0, 256), (256, 256), (512, 512), (1024, 512), (1536, 512), (2048, 512), (2560, 512), (3072, 512), (3584, 256),
       (3840, 128), (3968, 128)]
-TWO = (5, 6, 7)
+TWO = (3, 4, 5, 6, 7)
+YS = (12, 4)
 ORDER = {
-    "V": "0.0 0.1 2.1 0.2 2.2 1.1 0.3 1.2 3.1 1.3 2.3 1.r 4.1 3.2 4.2 3.3 5.2 4.3 5.3 6.2 8.1 6.3 7.2 9.1 7.3 9.2 8.2 10.1 "
-         "8.3 10.2 8.r 10.3 9.3 10.r 9.r",
-    "S": "2.0 5.0 1.0 3.0 5.1 4.0 6.0 0.r 6.1 2.r 7.1 7.0 0.t 10.0 9.0 3.r 1.t 8.0 4.r 5.r 3.t 2.t 6.r 4.t 7.r 6.t 5.t 7.t "
-         "8.t 10.t 9.t",
-    "P": "0.m 1.m 2.m 3.m 4.m 5.m 6.m 7.m 8.m 10.m 9.m",
-    "G": "5.+ 6.+ 7.+"}
-NB = 6
+    "V": "mpg pm mpr0 snd0 xe0 xe2 xe4 mpr1 x0A0 x0A2 pmf mpf idx perm0 perm1 l0 b1 "
+         "A00 A10 A20 A30 A40 A50 snd1 A60 A70 A0e A2e A4e A6e A8e x1A0 x1A2 aqs l1 ld "
+         "10.0 1.0 0.1 1.1 0.2 1.2 0.3 1.3 2.1 0.r 2.2 10.1 1.r 10.2 2.3 10.3 3.2 4.2 3.3 4.3 5.2 6.2 5.3 6.3 7.2 8.1 7.3 "
+         "8.2 7.r 9.1 8.3 9.2 8.r 9.3 9.r so ldo st wv",
+    "S": "xe1 xe3 x0A4 x0A1 ldb x0A3 permb b0 "
+         "A02 A12 A22 A32 A42 A52 A62 A72 A1e A3e A5e A7e x1A4 x1A1 x1A3 q0 q1 q2 q3 "
+         "0.0 3.0 2.0 4.0 5.0 6.0 2.r 10.r 7.0 3.r 10.t 4.r 2.t 9.0 8.0 5.r 6.r 0.t 3.t 5.t 4.t 6.t 7.t 8.t 9.t eo wmB et",
+    "P": "px0 px1 px2 px3 px4 pld pidx pm1 pm0 pb1 pb0 A0m A1m A2m A3m A4m A5m A6m A7m A8m pbd paq "
+         "0.m 10.m 2.m 3.m 4.m 5.m 6.m 7.m 8.m 9.m pso pst",
+    "G": "cn lb pio saq r16 s0A l32 gi s1A 3.+ 4.+ 5.+ 6.+ 7.+ ssB",
+    "Y": "aq aw"}
+ROT = (0, 1, 2, 3, 4, 5)
+FIRST = ["idx", "perm0", "b0", "ldb", "perm1", "b1"]
+SEMAPHORES = ["cV", "cS", "cP", "cG", "dx", "dx2", "dxr", "dsnd", "dmp", "dsrc", "daq", "dbs", "daw", "dql", "gi", "st0", "st1",
+              "dw", "aqa", "arr0A", "arr1A", "scB0", "scB1", "scB2", "scB3", "loc", "rq", "r1A"]
+SEMAPHORES += ["ac%d" % _j for _j in TWO]
 
 
 def rank_program(g, core, T, topo):
-    r = T.rank_of(core)
+    helper = {c: [k for k in topo.cores_of(c) if topo.die(k) != topo.die(c)][0] for c in T.cores}
+    served = {k: c for c, k in helper.items()}
+    r = T.rank_of(served.get(core, core))
     if r is None:
         return
     A, F = AluOpType, ActivationFunctionType
     queues = {"V": g.vector, "S": g.scalar, "P": g.tensor, "G": g, "Y": g.sync}
+    V, S = g.vector, g.scalar
     cnt = {"V": 0, "S": 0, "P": 0, "G": 0}
-    seen = {}
-    total = {}
+    seen, total, tasks, ready, later = {}, {}, {}, {}, {}
+    order = {q: ORDER[q].split() for q in ORDER}
 
     def wait(q, *tokens):
-        for t in tokens:
-            s, v = t
+        for s, v in tokens:
             if seen.get((q, s), 0) < v:
                 queues[q].wait_ge(T.sem[s], v)
                 seen[(q, s)] = v
@@ -62,10 +75,17 @@ def rank_program(g, core, T, topo):
         total[sem] = total.get(sem, 0) + 16
         return (sem, total[sem])
 
+    def task(name, deps, call):
+        tasks[name] = (deps, call)
+
+    def op(name, deps, call):
+        task(name, deps, lambda q: done(q, call()))
+
     peers = [T.cores[(r + k) % N] for k in (1, 2, 3)]
     ranks = [(r + k) % N for k in (1, 2, 3)]
     eng = len(topo.engines(core, peers[0]))
     nloc = [0]
+    slot = slice(E + CAP * r, E + CAP * r + CAP)
 
     def send(out, in_, sem, dst):
         rid, pid = topo.addr(dst, core)
@@ -81,14 +101,36 @@ def rank_program(g, core, T, topo):
                                               remote_sem=T.sem[sem], src=in_, dsts=[out, out, out])], local_sem=T.sem.loc)
         nloc[0] += eng
 
+    if core in served:
+        near = len(topo.engines(served[core], core))
+        g.wait_ge(T.sem.rq, near)
+        send_all(T.aql[r], T.aqd[:], "aqa")
+        g.wait_ge(T.sem.r1A, near)
+        send(T.w1[:, slot], T.sb1[:, 0:CAP], "arr1A", peers[0])
+        g.wait_ge(T.sem.loc, nloc[0])
+        return
+
     def bank(b, n, o=0):
         return T.ps[:, 512 * b + o:512 * b + o + n]
 
-    def gather(q, out, win, off, deps):
-        wait(q, *deps)
+    def mm(*a):
+        return done("P", g.tensor.matmul(*a))
+
+    def gather(q, out, win, off):
         if q == "V":
-            return done("V", g.vector.tensor_copy(out, win.indirect(off)))
-        return done("S", g.scalar.activation(out, win.indirect(off), F.Identity))
+            return done("V", V.tensor_copy(out, win.indirect(off)))
+        return done("S", S.activation(out, win.indirect(off), F.Identity))
+
+    def relu(q, out, in_, b):
+        if q == "V":
+            return done("V", V.tensor_scalar(out, in_, b, 0.0, A.add, A.max))
+        return done("S", S.activation(out, in_, F.Relu, bias=b))
+
+    turn = [x for x in order["P"] if x[-1] == "m"]
+    reader = {x: x[:-1] + ("t" if "." in x else "e") for x in turn}
+    rot = {x: i % 8 if i < len(P0) else ROT[(i - len(P0)) % len(ROT)] for i, x in enumerate(turn)}
+    free = {x: [reader[y] for y in turn[:i] if rot[y] == rot[x]][-1:] or FIRST for i, x in enumerate(turn)}
+    after0 = {b: [reader[y] for y in turn[:len(P0)] if rot[y] == b] for b in (6, 7)}
 
     tx = [dma("Y", "dx", T.xs[:, 0:XP // 2], T.x[:, 0:XP // 2]), dma("Y", "dx2", T.xs[:, XP // 2:XP], T.x[:, XP // 2:XP])]
     dma("S", "daq", T.aqd[0:16, :], T.aq[:])
@@ -99,260 +141,199 @@ def rank_program(g, core, T, topo):
         txr = dma("YS"[k % 2], "dxr", T.w0[16 * k:16 * k + 16, XP:E], T.x[:, XP:E])
     tsrc = dma("Y", "dsrc", T.l0i[:], T.src[:])
     tbs = dma("Y", "dbs", T.bst[:], T.bs[:])
-    dma("Y", "daw", T.abt[:], T.ab[:])
-    for k in range(8):
-        taw = dma("Y", "daw", T.awr[:, 16 * k:16 * k + 16], T.aw[:])
+    onesb = done("V", V.memset(T.onesb[:], 1.0))
+    c16 = done("V", V.memset(T.c16[:], 16.0))
+    ones = done("V", V.memset(T.ones[:], 1.0))
+    zero = done("V", V.memset(T.awb[:], 0.0))
 
-    v1 = done("V", g.vector.memset(T.onesb[:], 1.0))
-    v2 = done("V", g.vector.memset(T.c16[:], 16.0))
-    v3 = done("V", g.vector.memset(T.ones[:], 1.0))
-    wait("G", v1)
-    tlb = done("G", g.affine_select(T.lb[:], T.onesb[0:16, :], [[0, 8], [1, 16]], A.is_equal, 0.0, 0, -1))
-    wait("G", v2)
-    t = done("G", g.affine_select(T.r16a[:], T.c16[:], [[1, 128]], A.is_ge, 0.0, 0, -16))
-    wait("G", t)
-    tr16 = done("G", g.affine_select(T.r16[:], T.r16a[:], [[-1, 128]], A.is_ge, 0.0, 15, 16))
-    tpio = done("G", g.iota(T.pio[:], [[0, 1]], 0, 1))
-    tcn = done("G", g.iota(T.cn[:], [[0, 8], [-1, 16]], 0, 1, allow_small_or_imprecise_dtypes=True))
-    wait("G", taq)
-    send_all(T.aql[r], T.aqd[:], "aqa")
+    def load_aw(q):
+        for k in range(8):
+            dma(q, "daw", T.awb[16 * k:16 * k + 16, 16 * k:16 * k + 16], T.aw[:])
+            t = dma(q, "daw", T.abc[16 * k:16 * k + 16, :], T.ab[:])
+        return t
+    task("aw", [zero], load_aw)
 
-    wait("P", tlb)
-    px = []
+    op("lb", [onesb], lambda: g.affine_select(T.lb[:], T.onesb[0:16, :], [[0, 8], [1, 16]], A.is_equal, 0.0, 0, -1))
+    op("l32", [ones], lambda: g.affine_select(T.l32[:], T.ones[:], [[0, 8], [1, 16]], A.is_equal, 0.0, 0, -1))
+    op("r16", [c16], lambda: g.affine_select(T.r16[:], T.c16[:], [[1, 8], [0, 16]], A.is_equal, 0.0, 0, -1))
+    op("pio", [], lambda: g.iota(T.pio[:], [[0, 1]], 0, 1))
+    op("cn", [], lambda: g.iota(T.cn[:], [[0, 8], [-1, 16]], 0, 1, allow_small_or_imprecise_dtypes=True))
+    task("saq", [taq], lambda q: send(T.aqd[:], T.aqd[:], "rq", helper[core]))
+
+    xe = ["xe%d" % b for b in range(XP // 512)]
     for b in range(XP // 512):
-        wait("P", tx[512 * b >= XP // 2])
-        px.append(done("P", g.tensor.matmul(bank(b, 512), T.lb[:], T.xs[:, 512 * b:512 * b + 512], True, True)))
-    wait("V", tsnd)
-    vsnd = done("V", g.vector.tensor_copy(T.snd0[:], T.snd0i[:]))
-    xe = []
-    for b in range(XP // 512):
-        q = "VS"[b % 2]
-        wait(q, px[b])
-        o = T.w0[:, 512 * b:512 * b + 512]
-        if q == "V":
-            xe.append(done("V", g.vector.tensor_copy(o, bank(b, 512))))
-        else:
-            xe.append(done("S", g.scalar.activation(o, bank(b, 512), F.Identity)))
+        task("px%d" % b, ["lb", tx[0], tx[512 * b + 512 > XP // 2]],
+             lambda q, b=b: mm(bank(b, 512), T.lb[:], T.xs[:, 512 * b:512 * b + 512], True, True))
+        task(xe[b], ["px%d" % b], lambda q, b=b: done(q, V.tensor_copy(T.w0[:, 512 * b:512 * b + 512], bank(b, 512)) if q == "V" else
+                                                      S.activation(T.w0[:, 512 * b:512 * b + 512], bank(b, 512), F.Identity)))
 
-    def exchange(win, sb, lists, deps, sem):
-        w = win[:, 0:E]
-        tk = []
-        for i, q, o, n in ((0, "V", 0, 128), (0, "S", 128, 128), (1, "V", 0, 256), (2, "S", 0, 256)):
-            c0 = 16 * ranks[i] + o // 16
-            tk.append((i, gather(q, sb[:, CAP * i + o:CAP * i + o + n], w, lists[:, c0:c0 + n // 16], deps)))
-        own = gather("S", win[:, E + CAP * r:E + CAP * r + CAP], w, lists[:, 16 * r:16 * r + 16], deps)
-        for i in range(3):
-            wait("G", *[t for j, t in tk if j == i])
-            send(win[:, E + CAP * r:E + CAP * r + CAP], sb[:, CAP * i:CAP * i + CAP], sem, peers[i])
-        return own
+    perm = (T.perm0, T.perm1)
+    op("mpf", [tmp], lambda: V.tensor_copy(T.mpf[:], T.mpi[:]))
+    op("mpg", [tmp], lambda: V.tensor_copy(T.mpg[:], T.mpi[:]))
+    op("pm", ["pio"], lambda: V.tensor_scalar(T.pm[:], T.pio[:], 15, None, A.bitwise_and))
+    op("pmf", ["pm"], lambda: V.tensor_copy(T.pmf[:], T.pm[:]))
+    task("pidx", ["mpf", "r16"] + xe, lambda q: mm(bank(0, 1), T.r16[:], T.mpf[:, 1:2], True, True))
+    op("idx", ["pidx", "pmf"], lambda: V.tensor_scalar(T.idx[:], bank(0, 1), T.pmf[:], None, A.add))
+    for s in (0, 1):
+        op("mpr%d" % s, ["mpg"], lambda s=s: V.tensor_scalar(T["mpr%d" % s][:], T.onesb[0:8, :], T.mpg[:, s:s + 1], None, A.mult))
+        task("pm%d" % s, ["mpr%d" % s, "r16"] + xe, lambda q, s=s: mm(bank(1 + 3 * s, 128), T["mpr%d" % s][:], T.r16[:], True, True))
+        op("perm%d" % s, ["pm%d" % s, "cn"], lambda s=s: V.tensor_tensor(perm[s][:], bank(1 + 3 * s, 128), T.cn[:], A.is_equal))
+        task("pb%d" % s, ["perm%d" % s, tbs], lambda q, s=s: mm(bank(2 + 3 * s, 1), perm[s][:], T.bst[:], True, True))
+    op("permb", ["perm0"], lambda: S.activation(T.permb[:], T.perm0[:], F.Identity, scale=0.0625))
+    op("b0", ["pb0"], lambda: S.activation(T.b0[:], bank(2, 1), F.Identity, scale=0.25))
+    op("b1", ["pb1"], lambda: V.tensor_copy(T.b1[:], bank(5, 1)))
 
-    own0 = exchange(T.w0, T.sb0, T.snd0, xe + [vsnd, txr], "arr0")
+    def fetch(q):
+        for o, tab in ((T.snd1i, T.snd), (T.l1i, T.src)):
+            g.indirect_dma_start(o[:], None, tab[:], IndirectOffsetOnAxis(ap=T.idx[:], axis=0),
+                                 bounds_check=127).then_inc(T.sem.gi, 16)
+        total["gi"] = 32
+        return ("gi", 32)
+    task("gi", ["idx"], fetch)
+    op("snd0", [tsnd], lambda: V.tensor_copy(T.snd0[:], T.snd0i[:]))
+    op("snd1", ["gi"], lambda: V.tensor_copy(T.snd1[:], T.snd1i[:]))
+    for x, dep in (("l0", tsrc), ("l1", "gi")):
+        task(x, [dep], lambda q, x=x: [done("V", V.tensor_copy(T[x][:, :, 32 * d:32 * d + 32], T[x + "i"][:, 256 * d:256 * d + 256]))
+                                       for d in range(4)][3])
 
-    wait("V", tmp)
-    done("V", g.vector.tensor_copy(T.mpf[:], T.mpi[:]))
-    t3 = done("V", g.vector.tensor_copy(T.mpg[:], T.mpi[:]))
-    wait("V", tpio)
-    t2 = done("V", g.vector.tensor_scalar(T.pm[:], T.pio[:], 15, None, A.bitwise_and))
-    wait("V", t3)
-    tm = [done("V", g.vector.tensor_scalar(T.mpr0[:], T.onesb[0:8, :], T.mpg[:, 0:1], None, A.mult)),
-          done("V", g.vector.tensor_scalar(T.mpr1[:], T.onesb[0:8, :], T.mpg[:, 1:2], None, A.mult))]
-    wait("V", t2)
-    tpm = done("V", g.vector.tensor_copy(T.pmf[:], T.pm[:]))
-    wait("P", tr16, *tm)
-    wait("P", *xe)
-    pidx = done("P", g.tensor.matmul(bank(2, 2), T.r16[:], T.mpf[:], True, True))
-    pa = done("P", g.tensor.matmul(bank(0, 128), T.mpr0[:], T.r16[:], True, True))
-    wait("V", pidx, tpm)
-    tidx = done("V", g.vector.tensor_scalar(T.idx[:], bank(2, 2), T.pmf[:], None, A.add))
-    wait("V", tcn, pa)
-    t = done("V", g.vector.tensor_tensor(T.perm0[:], bank(0, 128), T.cn[:], A.is_equal))
-    wait("V", tsrc)
-    vl0 = done("V", g.vector.tensor_copy(T.l0[:], T.l0i[:]))
-    wait("S", t)
-    tpb = done("S", g.scalar.activation(T.permb[:], T.perm0[:], F.Identity, scale=0.0625))
-    wait("P", tbs, t)
-    t = done("P", g.tensor.matmul(bank(3, 1), T.perm0[:], T.bst[:], True, True))
-    wait("S", t)
-    tb0 = done("S", g.scalar.activation(T.b0[:], bank(3, 1), F.Identity, scale=0.25))
-    wait("G", tidx)
-    for o, tab in ((T.snd1i, T.snd), (T.l1i, T.src)):
-        g.indirect_dma_start(o[:], None, tab[:], IndirectOffsetOnAxis(ap=T.idx[:, 1:2], axis=0),
-                             bounds_check=127).then_inc(T.sem.gi, 16)
-    wait("G", v3)
-    t = done("G", g.affine_select(T.bda[:], T.ones[:], [[-16, 8], [0, 16]], A.is_ge, 0.0, 0, 1))
-    wait("G", t)
-    tbd = done("G", g.affine_select(T.bd[:], T.bda[:], [[16, 8], [0, 16]], A.is_ge, 0.0, 15, -1))
-    wait("Y", taq)
-    dma("Y", "dql", T.aq16[:, r:r + 1], T.aqd[0:16, :])
-    wait("Y", ("aqa", 3 * eng))
-    for q in ranks:
-        tql = dma("Y", "dql", T.aq16[:, q:q + 1], T.aql[q, 0:16, :])
-
-    bufs = (T.ga, T.gb, T.gg, T.gd)
-    chunks = [(0, 1024), (1024, 1024), (2048, 1024), (3072, 512), (3584, 256), (3840, 128), (3968, 128)]
-    arrived = [("arr0", 3 * eng), own0, vl0, txr] + xe
-    pend, h0, npiece = [], [], 0
-
-    def evac(p):
-        e0, n, b, q, tk = p
-        o, i = T.w1[:, e0:e0 + n], bank(b, n)
-        wait(q, tk, tb0)
-        if q == "V":
-            h0.append(done("V", g.vector.tensor_scalar(o, i, T.b0[:], 0.0, A.add, A.max)))
-        else:
-            h0.append(done("S", g.scalar.activation(o, i, F.Relu, bias=T.b0[:])))
-
-    for e0, n in chunks:
-        tk = [gather("VVSS"[d], bufs[d][:, e0:e0 + n], T.w0[:],
-                     T.l0[:, 256 * d + e0 // 16:256 * d + (e0 + n) // 16], arrived) for d in (0, 2, 1, 3)]
-        for p in pend:
-            evac(p)
-        pend = []
-        for c0 in range(e0, e0 + n, 512):
-            m = min(512, e0 + n - c0)
-            b = npiece % 8
-            wait("P", tpb, tb0)
-            if npiece >= 8:
-                wait("P", h0[npiece - 8])
-            for i, d in enumerate((0, 2, 1, 3)):
-                wait("P", tk[i])
-                x = done("P", g.tensor.matmul(bank(b, m), T.permb[:], bufs[d][:, c0:c0 + m], i == 0, i == 3))
-            pend.append((c0, m, b, "VS"[npiece % 2], x))
-            npiece += 1
-        if e0 == 1024:
-            wait("V", ("gi", 32))
-            vs1 = done("V", g.vector.tensor_copy(T.snd1[:], T.snd1i[:]))
-    for p in pend:
-        evac(p)
-
-    own1 = exchange(T.w1, T.sb1, T.snd1, h0 + [vs1], "arr1")
-
-    tl32 = done("V", g.vector.tensor_copy(T.l32[:], T.lb[:]))
-    vl1 = done("V", g.vector.tensor_copy(T.l1[:], T.l1i[:]))
-    wait("P", taw, tql, tl32)
-    wait("P", *h0)
-    p1 = done("P", g.tensor.matmul(bank(0, 128), T.l32[:], T.awr[:], True, True))
-    p2 = done("P", g.tensor.matmul(bank(1, 1), T.l32[:], T.abt[:], True, True))
-    p3 = done("P", g.tensor.matmul(bank(2, 16), T.l32[:], T.l32[:, 0:16], True, True))
-    p4 = done("P", g.tensor.matmul(bank(3, 4), T.l32[:], T.aq16[:], True, True))
-    p5 = done("P", g.tensor.matmul(bank(4, 128), T.mpr1[:], T.r16[:], True, True))
-    wait("S", p3)
-    tldb = done("S", g.scalar.activation(T.ldb[:], bank(2, 16), F.Tanh, scale=16.0))
-    wait("V", p5)
-    t = done("V", g.vector.tensor_tensor(T.perm1[:], bank(4, 128), T.cn[:], A.is_equal))
-    wait("P", t)
-    p6 = done("P", g.tensor.matmul(bank(5, 1), T.perm1[:], T.bst[:], True, True))
-    wait("V", p4)
-    t = done("V", g.vector.tensor_scalar(T.aqs[:], bank(3, 4), 2.0 ** -14, None, A.mult))
-    wait("V", p1, tbd)
-    tawb = done("V", g.vector.tensor_tensor(T.awb[:], bank(0, 128), T.bd[:], A.mult))
-    wait("V", p2)
-    tabc = done("V", g.vector.tensor_copy(T.abc[:], bank(1, 1)))
-    wait("V", tldb)
-    tl = done("V", g.vector.tensor_scalar(T.ld[:], T.ldb[:], -1.0, 1024.0, A.add, A.mult))
-    wait("V", p6)
-    tb1 = done("V", g.vector.tensor_copy(T.b1[:], bank(5, 1)))
-    wait("S", t, tbd)
+    def load_aq(q):
+        dma(q, "dql", T.aq16[:, r:r + 1], T.aqd[0:16, :])
+        wait(q, ("aqa", 3 * eng))
+        return [dma(q, "dql", T.aq16[:, k:k + 1], T.aql[k, 0:16, :]) for k in ranks][2]
+    task("aq", [taq], load_aq)
+    task("paq", ["aq", "l32"] + after0[6], lambda q: mm(bank(6, 4), T.l32[:], T.aq16[:], True, True))
+    op("aqs", ["paq"], lambda: V.tensor_scalar(T.aqs[:], bank(6, 4), 2.0 ** -22, None, A.mult))
+    task("pbd", ["r16"] + after0[7], lambda q: mm(bank(7, 128), T.r16[:], T.r16[:], True, True))
     qs = (T.q0, T.q1, T.q2, T.q3)
-    for q in range(N):
-        tq = done("S", g.scalar.activation(qs[q][:], T.bd[:], F.Identity, scale=T.aqs[:, q:q + 1]))
+    for k in range(N):
+        op("q%d" % k, ["pbd", "aqs"], lambda k=k: S.activation(qs[k][:], bank(7, 128), F.Identity, scale=T.aqs[:, k:k + 1]))
+    task("pld", ["lb"] + xe, lambda q: mm(bank(3, 16), T.lb[:], T.lb[:, 0:16], True, True))
+    op("ldb", ["pld"], lambda: S.activation(T.ldb[:], bank(3, 16), F.Tanh, scale=16.0))
+    op("ld", ["ldb"], lambda: V.tensor_scalar(T.ld[:], T.ldb[:], -1.0, 1024.0, A.add, A.mult))
 
-    arrived = [("arr1", 3 * eng), own1, vl1] + h0
-    ready = {}
-    pord = [int(x.split(".")[0]) for x in ORDER["P"].split()]
+    def exchange(x, win, sb, lists, deps, relay):
+        parts = [(0, 0, 0, 128), (4, 0, 128, 128), (1, 1, 0, CAP), (2, 2, 0, CAP)]
+        for j, i, o, n in parts:
+            c = 16 * ranks[i] + o // 16
+            task("x%s%d" % (x, j), deps, lambda q, i=i, o=o, n=n, c=c:
+                 gather(q, sb[:, CAP * i + o:CAP * i + o + n], win[:, 0:E], lists[:, c:c + n // 16]))
+        task("x%s3" % x, deps, lambda q: gather(q, win[:, slot], win[:, 0:E], lists[:, 16 * r:16 * r + 16]))
 
-    def needs(j, k):
-        if k == "0" or k == "1" and j in TWO:
-            return []
-        if k == "+":
-            return [(j, "0"), (j, "1")]
-        if k == "m":
-            i = pord.index(j)
-            return [(j, "r")] + ([(pord[i - NB], "t")] if i >= NB else [])
-        before = {"1": "0", "2": "+" if j in TWO else "1", "3": "2", "r": "3", "t": "m"}
-        return [(j, before[k])]
+        def sends(q):
+            for i in range(3):
+                wait(q, *[ready["x%s%d" % (x, j)] for j, k, o, n in parts if k == i])
+                if relay and i == 0:
+                    send(sb[:, 0:CAP], sb[:, 0:CAP], "r" + x, helper[core])
+                else:
+                    send(win[:, slot], sb[:, CAP * i:CAP * i + CAP], "arr" + x, peers[i])
+        task("s" + x, [], sends)
+        later["s" + x] = ["x%s%d" % (x, p[0]) for p in parts]
 
-    def emit(q, j, k):
-        e0, n = CH[j]
-        s = slice(e0, e0 + n)
-        wait(q, *[ready[x] for x in needs(j, k)])
-        sums = (T.a0, T.a0, T.a1, T.a0) if j in TWO else (T.a0, T.a1, T.a0, T.a1)
-        if k in "0123":
-            off = T.l1[:, 256 * int(k) + e0 // 16:256 * int(k) + (e0 + n) // 16]
-            if k == "0" or k == "1" and j in TWO:
-                return gather(q, (T.a0 if k == "0" else T.h)[:, s], T.w1[:], off, arrived)
-            wait("V", *arrived)
-            return done("V", g.vector.tensor_tensor(sums[int(k)][:, s], T.w1[:].indirect(off), sums[int(k) - 1][:, s], A.add))
-        if k == "+":
-            sem = "ac%d" % j
-            g.dma_start(T.a0[:, s], T.h[:, s], accum_op=A.add).then_inc(T.sem[sem], 16)
-            total[sem] = 16
-            return (sem, 16)
-        if k == "r":
-            wait(q, tb1)
-            if q == "V":
-                return done("V", g.vector.tensor_scalar(T.h[:, s], sums[3][:, s], T.b1[:], 0.0, A.add, A.max))
-            return done("S", g.scalar.activation(T.h[:, s], sums[3][:, s], F.Relu, bias=T.b1[:]))
-        b = bank(pord.index(j) % NB, n)
-        if k == "m":
-            wait("P", tawb, tb1, tq)
-            return done("P", g.tensor.matmul(b, T.awb[:], T.h[:, s], True, True))
-        wait("S", tabc)
-        return done("S", g.scalar.activation(T.th[:, s], b, F.Tanh, bias=T.abc[:],
-                                             accum_out=T.acc[:, 12 * r + j:12 * r + j + 1]))
+    h0 = ["A%de" % j for j in range(len(P0))]
+    exchange("0A", T.w0, T.sb0, T.snd0, xe + ["snd0", txr], False)
+    exchange("1A", T.w1, T.sb1, T.snd1, h0 + ["snd1"], True)
 
-    left = {q: [(int(x.split(".")[0]), x.split(".")[1]) for x in ORDER[q].split()] for q in "VSPG"}
+    for b in range(8):
+        for x, d, k in ((4, 0, 4), (0, 0, 2), (2, 2, 2)):
+            task("A%d%d" % (b, x), [("arr0A", 3 * eng), "x0A3", "l0", txr] + xe, lambda q, b=b, d=d, k=k:
+                 gather(q, T.gb[:, b, 512 * d:512 * (d + k)], T.w0[:], T.l0[:, b, 32 * d:32 * (d + k)]))
+    for j, (e0, n) in enumerate(P0):
+        name, b = "A%dm" % j, e0 // 512
+        later[name] = ["A%d4" % b] * 2 if "A%d4" % b in order["V"] + order["S"] else ["A%d0" % b, "A%d2" % b]
+
+        def add4(q, name=name, b=b, o=e0 % 512, n=n):
+            for d in range(4):
+                wait(q, ready[later[name][d // 2]])
+                t = mm(bank(rot[name], n), T.permb[:], T.gb[:, b, 512 * d + o:512 * d + o + n], d == 0, d == 3)
+            return t
+        task(name, ["permb"] + free[name], add4)
+        task(h0[j], [name, "b0"], lambda q, name=name, e0=e0, n=n: relu(q, T.w1[:, e0:e0 + n], bank(rot[name], n), T.b0[:]))
+
+    arrived = [("arr1A", 3 * eng), "x1A3", "l1"] + h0
+    adds = [j for j in TWO if "%d.+" % j in order["G"]]
+    for j, (v, n) in enumerate(G1):
+        two, b, o = j in TWO, v // 512, v % 512
+        a0, a1 = T.a0[:, b, o:o + n], T.a1[:, v:v + n]
+        sums = (a0, a0, a1, a0) if two else (a0, a1, a0, a1)
+        head = max([c for c in adds if c <= j] + [0])
+        b1 = min([G1[c][0] // 512 for c in adds if c > j] + [G1[TWO[-1]][0] // 512 + 1])
+        task("%d.0" % j, arrived, lambda q, b=b, o=o, m=1024 if two else n:
+             gather(q, T.a0[:, b, o:o + m], T.w1[:], T.l1[:, b, o // 16:(o + m) // 16]))
+        for d in range(1 + two, 4):
+            op("%d.%d" % (j, d), arrived + ["%d.+" % head if d == 2 and two else "%d.%d" % (j, d - 1)],
+               lambda d=d, sums=sums, off=T.l1[:, b, 32 * d + o // 16:32 * d + (o + n) // 16]:
+               V.tensor_tensor(sums[d], T.w1[:].indirect(off), sums[d - 1], A.add))
+
+        def add2(q, j=j, b=b, b1=b1):
+            g.dma_start(T.a0[:, b:b1, 0:512], T.a0[:, b:b1, 512:1024], accum_op=A.add).then_inc(T.sem["ac%d" % j], 16)
+            total["ac%d" % j] = 16
+            return ("ac%d" % j, 16)
+        task("%d.+" % j, ["%d.0" % [c[0] for c in G1].index(512 * k) for k in range(b, b1) if two], add2)
+        task("%d.r" % j, ["%d.3" % j, "b1"], lambda q, s=slice(v, v + n), x=sums[3]: relu(q, T.h[:, s], x, T.b1[:]))
+    heads = [j for j in range(len(G1)) if "%d.m" % j in turn]
+    for i, (j, k) in enumerate(zip(heads, heads[1:] + [len(G1)])):
+        s = slice(G1[j][0], sum(G1[k - 1]))
+        n = s.stop - s.start
+        task("%d.m" % j, ["%d.r" % c for c in range(j, k)] + ["aw"] + free["%d.m" % j],
+             lambda q, j=j, s=s, n=n: mm(bank(rot["%d.m" % j], n), T.awb[:], T.h[:, s], True, True))
+        op("%d.t" % j, ["%d.m" % j, "aw"], lambda i=i, j=j, s=s, n=n: S.activation(
+            T.th[:, s], bank(rot["%d.m" % j], n), F.Tanh, bias=T.abc[:], accum_out=T.acc[:, 16 * r + i:16 * r + i + 1]))
+
+    nch = len(heads)
+    tanh = ["%d.t" % j for j in heads]
+    qn = ["q%d" % k for k in range(N)]
+
+    def sums_of(k):
+        return T.acc[:, 16 * k:16 * k + nch]
+    task("ssB", tanh, lambda q: send_all(sums_of(r), sums_of(r), "scB%d" % r))
+    task("pso", tanh + qn, lambda q: mm(bank(6, nch), qs[r][:], sums_of(r), True, True))
+
+    def peers_sums(q):
+        for i, k in enumerate(ranks[::-1]):
+            wait(q, ("scB%d" % k, eng))
+            t = mm(bank(7, nch), qs[k][:], sums_of(k), i == 0, i == 2)
+        return t
+    task("pst", qn, peers_sums)
+    op("so", ["pso"], lambda: V.tensor_reduce(T.so[:], bank(6, nch), AxisListType.X, A.add))
+    op("eo", ["so"], lambda: S.activation(T.eo[:], T.so[:], F.Exp))
+    op("ldo", ["so", "ld"], lambda: V.tensor_scalar(T.ldo[:], T.ld[:], T.so[:], None, A.add))
+    op("st", ["pst"], lambda: V.tensor_reduce(T.st[:], bank(7, nch), AxisListType.X, A.add))
+    op("wmB", ["st", "ldo"], lambda: S.activation(T.wm[:], T.ldo[:], F.Exp, bias=T.st[:]))
+    op("et", ["st"], lambda: S.activation(T.et[:], T.st[:], F.Exp))
+    op("wv", ["et", "eo"], lambda: V.tensor_tensor(T.wv[:], T.et[:], T.eo[:], A.mult))
+
+    left = {q: list(order[q]) for q in order}
     while any(left.values()):
-        for q in "VSPG":
-            while left[q] and all(x in ready for x in needs(*left[q][0])):
+        before = sum(len(x) for x in left.values())
+        for q in left:
+            while left[q] and all(d in ready for d in tasks[left[q][0]][0] + later.get(left[q][0], []) if isinstance(d, str)):
                 x = left[q].pop(0)
-                ready[x] = last = emit(q, *x)
+                wait(q, *[ready[d] if isinstance(d, str) else d for d in tasks[x][0]])
+                ready[x] = tasks[x][1](q)
+        assert sum(len(x) for x in left.values()) < before, [x[:1] for x in left.values()]
 
-    nch = len(CH)
-    last = ("cS", cnt["S"])
-    wait("G", last)
-    mine = T.acc[:, 12 * r:12 * r + nch]
-    send_all(mine, mine, "sca%d" % r)
-    wait("P", last, tq)
-    p1 = done("P", g.tensor.matmul(bank(6, nch), qs[r][:], mine, True, True))
-    for i, q in enumerate(ranks[::-1]):
-        wait("P", ("sca%d" % q, eng))
-        p2 = done("P", g.tensor.matmul(bank(7, nch), qs[q][:], T.acc[:, 12 * q:12 * q + nch], i == 0, i == 2))
-    wait("V", p1)
-    t = done("V", g.vector.tensor_reduce(T.so[:], bank(6, nch), AxisListType.X, A.add))
-    wait("S", t)
-    teo = done("S", g.scalar.activation(T.eo[:], T.so[:], F.Exp))
-    wait("V", t, tl)
-    tld = done("V", g.vector.tensor_scalar(T.ldo[:], T.ld[:], T.so[:], None, A.add))
-    wait("V", p2)
-    t = done("V", g.vector.tensor_reduce(T.st[:], bank(7, nch), AxisListType.X, A.add))
-    wait("S", t, tld)
-    twm = done("S", g.scalar.activation(T.wm[:], T.ldo[:], F.Exp, bias=T.st[:]))
-    tet = done("S", g.scalar.activation(T.et[:], T.st[:], F.Exp))
-    wait("V", tet, teo)
-    twv = done("V", g.vector.tensor_tensor(T.wv[:], T.et[:], T.eo[:], A.mult))
-
-    wait("P", twm)
-    tz = []
-    for hb in (0, 1):
-        for b in range(8):
-            if hb:
-                wait("P", tz[b])
+    wait("P", ready["wmB"])
+    tz, e0 = [], 0
+    for grp, st in enumerate(YS):
+        y0 = e0 // 8
+        for b in range(st):
+            if len(tz) >= 8:
+                wait("P", tz[-8])
             for k in (0, 1):
-                c0 = 1024 * (2 * hb + k)
-                py = done("P", g.tensor.matmul(bank(b, 16, 16 * k), T.h[:, c0 + b:c0 + 1024:8], T.wm[:], True, True))
-            wait("V", py)
-            ty = done("V", g.vector.transpose(T.yt[:, 256 * hb + b:256 * hb + 256:8], bank(b, 32)))
-            tz.append(ty)
+                c0 = e0 + 128 * st * k
+                t = mm(bank(len(tz) % 8, 16, 16 * k), T.h[:, c0 + b:c0 + 128 * st:st], T.wm[:], True, True)
+            wait("V", t)
+            tz.append(done("V", V.transpose(T.yt[:, y0 + b:y0 + 32 * st:st], bank(len(tz) % 8, 32))))
         for a in range(4):
             for k in (0, 1):
                 q = "YS"[k]
-                wait(q, ty)
-                c0 = 1024 * (2 * hb + k) + 256 * a
-                dma(q, "st%d" % hb, T.y[:, c0:c0 + 256], T.yt[32 * a + 16 * k:32 * a + 16 * k + 16, 256 * hb:256 * hb + 256])
-        if hb == 0:
-            wait("Y", twv)
+                wait(q, tz[-1])
+                c0 = e0 + 128 * st * k + 32 * st * a
+                dma(q, "st%d" % grp, T.y[:, c0:c0 + 32 * st], T.yt[32 * a + 16 * k:32 * a + 16 * k + 16, y0:y0 + 32 * st])
+        if grp == 0:
+            wait("Y", ready["wv"])
             dma("Y", "dw", T.w[:], T.wv[0:128:16, :])
+        e0 += 256 * st
 
-    wait("G", ("loc", nloc[0]), ("gi", 32), *total.items())
-    wait("G", *[("c" + q, n) for q, n in cnt.items()])
+    wait("G", ("loc", nloc[0]), *[("c" + q, n) for q, n in cnt.items()])
+    wait("G", *total.items())

from concourse.bass import DstId, RemoteDMATransfer, IndirectOffsetOnAxis
from concourse.mybir import AluOpType, AxisListType, ActivationFunctionType

E, CAP, N = 4096, 256, 4
P = E + N * CAP
XP = 2560
SCRATCH = {"aqd": ("dram", [128, 1], "float32"), "aql": ("dram", [4, 128, 1], "float32"),
           "ps": ("psum", [128, 4096], "float32"), "l1": ("sbuf", [128, 8, 128], "uint16"),
           "l0": ("sbuf", [128, 8, 128], "uint16"), "gb": ("sbuf", [128, 8, 2048], "bfloat16"),
           "a0": ("sbuf", [128, 8, 1024], "float32")}
for _rows, _cols, _dt, _names in (
        (128, 128, "bfloat16", "onesb permb"), (8, 128, "bfloat16", "c16 r16 mpr0 mpr1"), (16, 128, "bfloat16", "lb"),
        (16, 128, "float32", "l32 ones"), (128, 128, "float32", "cn perm0 perm1 awb q0 q1 q2 q3"),
        (128, 1, "int32", "pio pm idx"), (128, 1, "float32", "pmf bst b0 b1 abc so st eo et wv"), (8, 2, "int32", "mpi"),
        (8, 2, "bfloat16", "mpf"), (8, 2, "float32", "mpg"),
        (16, 4, "float32", "aq16"), (16, XP, "bfloat16", "xs"), (128, 64, "int32", "snd0i snd1i"),
        (128, 64, "uint16", "snd0 snd1"), (128, 1024, "int32", "l0i l1i"),
        (128, P, "bfloat16", "w0"), (128, P, "float32", "w1"), (128, 3 * CAP, "bfloat16", "sb0"),
        (128, 3 * CAP, "float32", "sb1"), (128, E, "bfloat16", "th"), (128, E, "float32", "a1 h"),
        (128, 64, "float32", "acc"), (128, 16, "float32", "ld ldo wm"), (128, 16, "bfloat16", "ldb"),
        (128, 4, "float32", "aqs"), (128, 512, "float32", "yt")):
    for _n in _names.split():
        SCRATCH[_n] = ("sbuf", [_rows, _cols], _dt)

P0 = [(512 * _b, 512) for _b in range(7)] + [(3584, 448), (4032, 64)]
G1 = [(0, 256), (256, 256), (512, 512), (1024, 512), (1536, 512), (2048, 512), (2560, 512), (3072, 512), (3584, 256),
      (3840, 128), (3968, 128)]
TWO = (3, 4, 5, 6, 7)
YS = (12, 4)
ORDER = {
    "V": "mpg pm mpr0 snd0 xe0 xe2 xe4 mpr1 x0A0 x0A2 pmf mpf idx perm0 perm1 l0 b1 "
         "A00 A10 A20 A30 A40 A50 snd1 A60 A70 A0e A2e A4e A6e A8e x1A0 x1A2 aqs l1 ld "
         "10.0 1.0 0.1 1.1 0.2 1.2 0.3 1.3 2.1 0.r 2.2 10.1 1.r 10.2 2.3 10.3 3.2 4.2 3.3 4.3 5.2 6.2 5.3 6.3 7.2 8.1 7.3 "
         "8.2 7.r 9.1 8.3 9.2 8.r 9.3 9.r so ldo st wv",
    "S": "xe1 xe3 x0A4 x0A1 ldb x0A3 permb b0 "
         "A02 A12 A22 A32 A42 A52 A62 A72 A1e A3e A5e A7e x1A4 x1A1 x1A3 q0 q1 q2 q3 "
         "0.0 3.0 2.0 4.0 5.0 6.0 2.r 10.r 7.0 3.r 10.t 4.r 2.t 9.0 8.0 5.r 6.r 0.t 3.t 5.t 4.t 6.t 7.t 8.t 9.t eo wmB et",
    "P": "px0 px1 px2 px3 px4 pld pidx pm1 pm0 pb1 pb0 A0m A1m A2m A3m A4m A5m A6m A7m A8m pbd paq "
         "0.m 10.m 2.m 3.m 4.m 5.m 6.m 7.m 8.m 9.m pso pst",
    "G": "cn lb pio saq r16 s0A l32 gi s1A 3.+ 4.+ 5.+ 6.+ 7.+ ssB",
    "Y": "aq aw"}
ROT = (0, 1, 2, 3, 4, 5)
FIRST = ["idx", "perm0", "b0", "ldb", "perm1", "b1"]
SEMAPHORES = ["cV", "cS", "cP", "cG", "dx", "dx2", "dxr", "dsnd", "dmp", "dsrc", "daq", "dbs", "daw", "dql", "gi", "st0", "st1",
              "dw", "aqa", "arr0A", "arr1A", "scB0", "scB1", "scB2", "scB3", "loc", "rq", "r1A"]
SEMAPHORES += ["ac%d" % _j for _j in TWO]


def rank_program(g, core, T, topo):
    helper = {c: [k for k in topo.cores_of(c) if topo.die(k) != topo.die(c)][0] for c in T.cores}
    served = {k: c for c, k in helper.items()}
    r = T.rank_of(served.get(core, core))
    if r is None:
        return
    A, F = AluOpType, ActivationFunctionType
    queues = {"V": g.vector, "S": g.scalar, "P": g.tensor, "G": g, "Y": g.sync}
    V, S = g.vector, g.scalar
    cnt = {"V": 0, "S": 0, "P": 0, "G": 0}
    seen, total, tasks, ready, later = {}, {}, {}, {}, {}
    order = {q: ORDER[q].split() for q in ORDER}

    def wait(q, *tokens):
        for s, v in tokens:
            if seen.get((q, s), 0) < v:
                queues[q].wait_ge(T.sem[s], v)
                seen[(q, s)] = v

    def done(q, ins):
        ins.then_inc(T.sem["c" + q], 1)
        cnt[q] += 1
        return ("c" + q, cnt[q])

    def dma(q, sem, out, in_):
        queues[q].dma_start(out, in_).then_inc(T.sem[sem], 16)
        total[sem] = total.get(sem, 0) + 16
        return (sem, total[sem])

    def task(name, deps, call):
        tasks[name] = (deps, call)

    def op(name, deps, call):
        task(name, deps, lambda q: done(q, call()))

    peers = [T.cores[(r + k) % N] for k in (1, 2, 3)]
    ranks = [(r + k) % N for k in (1, 2, 3)]
    eng = len(topo.engines(core, peers[0]))
    nloc = [0]
    slot = slice(E + CAP * r, E + CAP * r + CAP)

    def send(out, in_, sem, dst):
        rid, pid = topo.addr(dst, core)
        g.remote_dma(out, in_, T.sem[sem], T.sem.loc, pid, rid, topo.mask(core, dst))
        nloc[0] += len(topo.engines(core, dst))

    def send_all(out, in_, sem):
        ids = []
        for d in peers:
            rid, pid = topo.addr(d, core)
            ids.append(DstId(rid=rid, pnc=pid))
        g.remote_dma_fused([RemoteDMATransfer(dst_ids=ids, dma_engine_mask=topo.mask(core, peers[0]),
                                              remote_sem=T.sem[sem], src=in_, dsts=[out, out, out])], local_sem=T.sem.loc)
        nloc[0] += eng

    if core in served:
        near = len(topo.engines(served[core], core))
        g.wait_ge(T.sem.rq, near)
        send_all(T.aql[r], T.aqd[:], "aqa")
        g.wait_ge(T.sem.r1A, near)
        send(T.w1[:, slot], T.sb1[:, 0:CAP], "arr1A", peers[0])
        g.wait_ge(T.sem.loc, nloc[0])
        return

    def bank(b, n, o=0):
        return T.ps[:, 512 * b + o:512 * b + o + n]

    def mm(*a):
        return done("P", g.tensor.matmul(*a))

    def gather(q, out, win, off):
        if q == "V":
            return done("V", V.tensor_copy(out, win.indirect(off)))
        return done("S", S.activation(out, win.indirect(off), F.Identity))

    def relu(q, out, in_, b):
        if q == "V":
            return done("V", V.tensor_scalar(out, in_, b, 0.0, A.add, A.max))
        return done("S", S.activation(out, in_, F.Relu, bias=b))

    turn = [x for x in order["P"] if x[-1] == "m"]
    reader = {x: x[:-1] + ("t" if "." in x else "e") for x in turn}
    rot = {x: i % 8 if i < len(P0) else ROT[(i - len(P0)) % len(ROT)] for i, x in enumerate(turn)}
    free = {x: [reader[y] for y in turn[:i] if rot[y] == rot[x]][-1:] or FIRST for i, x in enumerate(turn)}
    after0 = {b: [reader[y] for y in turn[:len(P0)] if rot[y] == b] for b in (6, 7)}

    tx = [dma("Y", "dx", T.xs[:, 0:XP // 2], T.x[:, 0:XP // 2]), dma("Y", "dx2", T.xs[:, XP // 2:XP], T.x[:, XP // 2:XP])]
    dma("S", "daq", T.aqd[0:16, :], T.aq[:])
    taq = dma("S", "daq", T.aqd[16:128, :], T.bs[16:128, :])
    tsnd = dma("Y", "dsnd", T.snd0i[:], T.snd[:])
    tmp = dma("S", "dmp", T.mpi[:], T.mp[:])
    for k in range(8):
        txr = dma("YS"[k % 2], "dxr", T.w0[16 * k:16 * k + 16, XP:E], T.x[:, XP:E])
    tsrc = dma("Y", "dsrc", T.l0i[:], T.src[:])
    tbs = dma("Y", "dbs", T.bst[:], T.bs[:])
    onesb = done("V", V.memset(T.onesb[:], 1.0))
    c16 = done("V", V.memset(T.c16[:], 16.0))
    ones = done("V", V.memset(T.ones[:], 1.0))
    zero = done("V", V.memset(T.awb[:], 0.0))

    def load_aw(q):
        for k in range(8):
            dma(q, "daw", T.awb[16 * k:16 * k + 16, 16 * k:16 * k + 16], T.aw[:])
            t = dma(q, "daw", T.abc[16 * k:16 * k + 16, :], T.ab[:])
        return t
    task("aw", [zero], load_aw)

    op("lb", [onesb], lambda: g.affine_select(T.lb[:], T.onesb[0:16, :], [[0, 8], [1, 16]], A.is_equal, 0.0, 0, -1))
    op("l32", [ones], lambda: g.affine_select(T.l32[:], T.ones[:], [[0, 8], [1, 16]], A.is_equal, 0.0, 0, -1))
    op("r16", [c16], lambda: g.affine_select(T.r16[:], T.c16[:], [[1, 8], [0, 16]], A.is_equal, 0.0, 0, -1))
    op("pio", [], lambda: g.iota(T.pio[:], [[0, 1]], 0, 1))
    op("cn", [], lambda: g.iota(T.cn[:], [[0, 8], [-1, 16]], 0, 1, allow_small_or_imprecise_dtypes=True))
    task("saq", [taq], lambda q: send(T.aqd[:], T.aqd[:], "rq", helper[core]))

    xe = ["xe%d" % b for b in range(XP // 512)]
    for b in range(XP // 512):
        task("px%d" % b, ["lb", tx[0], tx[512 * b + 512 > XP // 2]],
             lambda q, b=b: mm(bank(b, 512), T.lb[:], T.xs[:, 512 * b:512 * b + 512], True, True))
        task(xe[b], ["px%d" % b], lambda q, b=b: done(q, V.tensor_copy(T.w0[:, 512 * b:512 * b + 512], bank(b, 512)) if q == "V" else
                                                      S.activation(T.w0[:, 512 * b:512 * b + 512], bank(b, 512), F.Identity)))

    perm = (T.perm0, T.perm1)
    op("mpf", [tmp], lambda: V.tensor_copy(T.mpf[:], T.mpi[:]))
    op("mpg", [tmp], lambda: V.tensor_copy(T.mpg[:], T.mpi[:]))
    op("pm", ["pio"], lambda: V.tensor_scalar(T.pm[:], T.pio[:], 15, None, A.bitwise_and))
    op("pmf", ["pm"], lambda: V.tensor_copy(T.pmf[:], T.pm[:]))
    task("pidx", ["mpf", "r16"] + xe, lambda q: mm(bank(0, 1), T.r16[:], T.mpf[:, 1:2], True, True))
    op("idx", ["pidx", "pmf"], lambda: V.tensor_scalar(T.idx[:], bank(0, 1), T.pmf[:], None, A.add))
    for s in (0, 1):
        op("mpr%d" % s, ["mpg"], lambda s=s: V.tensor_scalar(T["mpr%d" % s][:], T.onesb[0:8, :], T.mpg[:, s:s + 1], None, A.mult))
        task("pm%d" % s, ["mpr%d" % s, "r16"] + xe, lambda q, s=s: mm(bank(1 + 3 * s, 128), T["mpr%d" % s][:], T.r16[:], True, True))
        op("perm%d" % s, ["pm%d" % s, "cn"], lambda s=s: V.tensor_tensor(perm[s][:], bank(1 + 3 * s, 128), T.cn[:], A.is_equal))
        task("pb%d" % s, ["perm%d" % s, tbs], lambda q, s=s: mm(bank(2 + 3 * s, 1), perm[s][:], T.bst[:], True, True))
    op("permb", ["perm0"], lambda: S.activation(T.permb[:], T.perm0[:], F.Identity, scale=0.0625))
    op("b0", ["pb0"], lambda: S.activation(T.b0[:], bank(2, 1), F.Identity, scale=0.25))
    op("b1", ["pb1"], lambda: V.tensor_copy(T.b1[:], bank(5, 1)))

    def fetch(q):
        for o, tab in ((T.snd1i, T.snd), (T.l1i, T.src)):
            g.indirect_dma_start(o[:], None, tab[:], IndirectOffsetOnAxis(ap=T.idx[:], axis=0),
                                 bounds_check=127).then_inc(T.sem.gi, 16)
        total["gi"] = 32
        return ("gi", 32)
    task("gi", ["idx"], fetch)
    op("snd0", [tsnd], lambda: V.tensor_copy(T.snd0[:], T.snd0i[:]))
    op("snd1", ["gi"], lambda: V.tensor_copy(T.snd1[:], T.snd1i[:]))
    for x, dep in (("l0", tsrc), ("l1", "gi")):
        task(x, [dep], lambda q, x=x: [done("V", V.tensor_copy(T[x][:, :, 32 * d:32 * d + 32], T[x + "i"][:, 256 * d:256 * d + 256]))
                                       for d in range(4)][3])

    def load_aq(q):
        dma(q, "dql", T.aq16[:, r:r + 1], T.aqd[0:16, :])
        wait(q, ("aqa", 3 * eng))
        return [dma(q, "dql", T.aq16[:, k:k + 1], T.aql[k, 0:16, :]) for k in ranks][2]
    task("aq", [taq], load_aq)
    task("paq", ["aq", "l32"] + after0[6], lambda q: mm(bank(6, 4), T.l32[:], T.aq16[:], True, True))
    op("aqs", ["paq"], lambda: V.tensor_scalar(T.aqs[:], bank(6, 4), 2.0 ** -22, None, A.mult))
    task("pbd", ["r16"] + after0[7], lambda q: mm(bank(7, 128), T.r16[:], T.r16[:], True, True))
    qs = (T.q0, T.q1, T.q2, T.q3)
    for k in range(N):
        op("q%d" % k, ["pbd", "aqs"], lambda k=k: S.activation(qs[k][:], bank(7, 128), F.Identity, scale=T.aqs[:, k:k + 1]))
    task("pld", ["lb"] + xe, lambda q: mm(bank(3, 16), T.lb[:], T.lb[:, 0:16], True, True))
    op("ldb", ["pld"], lambda: S.activation(T.ldb[:], bank(3, 16), F.Tanh, scale=16.0))
    op("ld", ["ldb"], lambda: V.tensor_scalar(T.ld[:], T.ldb[:], -1.0, 1024.0, A.add, A.mult))

    def exchange(x, win, sb, lists, deps, relay):
        parts = [(0, 0, 0, 128), (4, 0, 128, 128), (1, 1, 0, CAP), (2, 2, 0, CAP)]
        for j, i, o, n in parts:
            c = 16 * ranks[i] + o // 16
            task("x%s%d" % (x, j), deps, lambda q, i=i, o=o, n=n, c=c:
                 gather(q, sb[:, CAP * i + o:CAP * i + o + n], win[:, 0:E], lists[:, c:c + n // 16]))
        task("x%s3" % x, deps, lambda q: gather(q, win[:, slot], win[:, 0:E], lists[:, 16 * r:16 * r + 16]))

        def sends(q):
            for i in range(3):
                wait(q, *[ready["x%s%d" % (x, j)] for j, k, o, n in parts if k == i])
                if relay and i == 0:
                    send(sb[:, 0:CAP], sb[:, 0:CAP], "r" + x, helper[core])
                else:
                    send(win[:, slot], sb[:, CAP * i:CAP * i + CAP], "arr" + x, peers[i])
        task("s" + x, [], sends)
        later["s" + x] = ["x%s%d" % (x, p[0]) for p in parts]

    h0 = ["A%de" % j for j in range(len(P0))]
    exchange("0A", T.w0, T.sb0, T.snd0, xe + ["snd0", txr], False)
    exchange("1A", T.w1, T.sb1, T.snd1, h0 + ["snd1"], True)

    for b in range(8):
        for x, d, k in ((4, 0, 4), (0, 0, 2), (2, 2, 2)):
            task("A%d%d" % (b, x), [("arr0A", 3 * eng), "x0A3", "l0", txr] + xe, lambda q, b=b, d=d, k=k:
                 gather(q, T.gb[:, b, 512 * d:512 * (d + k)], T.w0[:], T.l0[:, b, 32 * d:32 * (d + k)]))
    for j, (e0, n) in enumerate(P0):
        name, b = "A%dm" % j, e0 // 512
        later[name] = ["A%d4" % b] * 2 if "A%d4" % b in order["V"] + order["S"] else ["A%d0" % b, "A%d2" % b]

        def add4(q, name=name, b=b, o=e0 % 512, n=n):
            for d in range(4):
                wait(q, ready[later[name][d // 2]])
                t = mm(bank(rot[name], n), T.permb[:], T.gb[:, b, 512 * d + o:512 * d + o + n], d == 0, d == 3)
            return t
        task(name, ["permb"] + free[name], add4)
        task(h0[j], [name, "b0"], lambda q, name=name, e0=e0, n=n: relu(q, T.w1[:, e0:e0 + n], bank(rot[name], n), T.b0[:]))

    arrived = [("arr1A", 3 * eng), "x1A3", "l1"] + h0
    adds = [j for j in TWO if "%d.+" % j in order["G"]]
    for j, (v, n) in enumerate(G1):
        two, b, o = j in TWO, v // 512, v % 512
        a0, a1 = T.a0[:, b, o:o + n], T.a1[:, v:v + n]
        sums = (a0, a0, a1, a0) if two else (a0, a1, a0, a1)
        head = max([c for c in adds if c <= j] + [0])
        b1 = min([G1[c][0] // 512 for c in adds if c > j] + [G1[TWO[-1]][0] // 512 + 1])
        task("%d.0" % j, arrived, lambda q, b=b, o=o, m=1024 if two else n:
             gather(q, T.a0[:, b, o:o + m], T.w1[:], T.l1[:, b, o // 16:(o + m) // 16]))
        for d in range(1 + two, 4):
            op("%d.%d" % (j, d), arrived + ["%d.+" % head if d == 2 and two else "%d.%d" % (j, d - 1)],
               lambda d=d, sums=sums, off=T.l1[:, b, 32 * d + o // 16:32 * d + (o + n) // 16]:
               V.tensor_tensor(sums[d], T.w1[:].indirect(off), sums[d - 1], A.add))

        def add2(q, j=j, b=b, b1=b1):
            g.dma_start(T.a0[:, b:b1, 0:512], T.a0[:, b:b1, 512:1024], accum_op=A.add).then_inc(T.sem["ac%d" % j], 16)
            total["ac%d" % j] = 16
            return ("ac%d" % j, 16)
        task("%d.+" % j, ["%d.0" % [c[0] for c in G1].index(512 * k) for k in range(b, b1) if two], add2)
        task("%d.r" % j, ["%d.3" % j, "b1"], lambda q, s=slice(v, v + n), x=sums[3]: relu(q, T.h[:, s], x, T.b1[:]))
    heads = [j for j in range(len(G1)) if "%d.m" % j in turn]
    for i, (j, k) in enumerate(zip(heads, heads[1:] + [len(G1)])):
        s = slice(G1[j][0], sum(G1[k - 1]))
        n = s.stop - s.start
        task("%d.m" % j, ["%d.r" % c for c in range(j, k)] + ["aw"] + free["%d.m" % j],
             lambda q, j=j, s=s, n=n: mm(bank(rot["%d.m" % j], n), T.awb[:], T.h[:, s], True, True))
        op("%d.t" % j, ["%d.m" % j, "aw"], lambda i=i, j=j, s=s, n=n: S.activation(
            T.th[:, s], bank(rot["%d.m" % j], n), F.Tanh, bias=T.abc[:], accum_out=T.acc[:, 16 * r + i:16 * r + i + 1]))

    nch = len(heads)
    tanh = ["%d.t" % j for j in heads]
    qn = ["q%d" % k for k in range(N)]

    def sums_of(k):
        return T.acc[:, 16 * k:16 * k + nch]
    task("ssB", tanh, lambda q: send_all(sums_of(r), sums_of(r), "scB%d" % r))
    task("pso", tanh + qn, lambda q: mm(bank(6, nch), qs[r][:], sums_of(r), True, True))

    def peers_sums(q):
        for i, k in enumerate(ranks[::-1]):
            wait(q, ("scB%d" % k, eng))
            t = mm(bank(7, nch), qs[k][:], sums_of(k), i == 0, i == 2)
        return t
    task("pst", qn, peers_sums)
    op("so", ["pso"], lambda: V.tensor_reduce(T.so[:], bank(6, nch), AxisListType.X, A.add))
    op("eo", ["so"], lambda: S.activation(T.eo[:], T.so[:], F.Exp))
    op("ldo", ["so", "ld"], lambda: V.tensor_scalar(T.ldo[:], T.ld[:], T.so[:], None, A.add))
    op("st", ["pst"], lambda: V.tensor_reduce(T.st[:], bank(7, nch), AxisListType.X, A.add))
    op("wmB", ["st", "ldo"], lambda: S.activation(T.wm[:], T.ldo[:], F.Exp, bias=T.st[:]))
    op("et", ["st"], lambda: S.activation(T.et[:], T.st[:], F.Exp))
    op("wv", ["et", "eo"], lambda: V.tensor_tensor(T.wv[:], T.et[:], T.eo[:], A.mult))

    left = {q: list(order[q]) for q in order}
    while any(left.values()):
        before = sum(len(x) for x in left.values())
        for q in left:
            while left[q] and all(d in ready for d in tasks[left[q][0]][0] + later.get(left[q][0], []) if isinstance(d, str)):
                x = left[q].pop(0)
                wait(q, *[ready[d] if isinstance(d, str) else d for d in tasks[x][0]])
                ready[x] = tasks[x][1](q)
        assert sum(len(x) for x in left.values()) < before, [x[:1] for x in left.values()]

    wait("P", ready["wmB"])
    tz, e0 = [], 0
    for grp, st in enumerate(YS):
        y0 = e0 // 8
        for b in range(st):
            if len(tz) >= 8:
                wait("P", tz[-8])
            for k in (0, 1):
                c0 = e0 + 128 * st * k
                t = mm(bank(len(tz) % 8, 16, 16 * k), T.h[:, c0 + b:c0 + 128 * st:st], T.wm[:], True, True)
            wait("V", t)
            tz.append(done("V", V.transpose(T.yt[:, y0 + b:y0 + 32 * st:st], bank(len(tz) % 8, 32))))
        for a in range(4):
            for k in (0, 1):
                q = "YS"[k]
                wait(q, tz[-1])
                c0 = e0 + 128 * st * k + 32 * st * a
                dma(q, "st%d" % grp, T.y[:, c0:c0 + 32 * st], T.yt[32 * a + 16 * k:32 * a + 16 * k + 16, y0:y0 + 32 * st])
        if grp == 0:
            wait("Y", ready["wv"])
            dma("Y", "dw", T.w[:], T.wv[0:128:16, :])
        e0 += 256 * st

    wait("G", ("loc", nloc[0]), *[("c" + q, n) for q, n in cnt.items()])
    wait("G", *total.items())
